import numpy as np
import ml_dtypes


def mxq(x, axis, fmt="e4m3"):
    dtype, down = {"e4m3": (ml_dtypes.float8_e4m3fn, 7), "e5m2": (ml_dtypes.float8_e5m2, 14)}[fmt]
    v = np.moveaxis(np.asarray(x, np.float32).astype(ml_dtypes.bfloat16).astype(np.float64), axis, -1)
    blocks = v.reshape(v.shape[:-1] + (-1, 32))
    amax = np.abs(blocks).max(-1, keepdims=True)
    byte = np.maximum(np.where(amax > 0, np.frexp(amax)[1] - 1 + 127, 0) - down, 1)
    scale = np.exp2(byte - 127.0)
    codes = (blocks / scale).astype(np.float32).astype(dtype).astype(np.float64)
    return np.moveaxis((codes * scale).reshape(v.shape), -1, axis)


WIDE = False


def mx_kscale(k):
    if not WIDE:
        return np.ones(k)
    levels = np.array([10, -10, 5, -5, 0])
    if k % 512:
        return np.exp2(np.random.permutation(np.resize(levels, k // 32))).repeat(32)
    a = np.empty((k // 512, 16))
    for p in range(k // 512):
        a[p, :8] = np.random.permutation(np.resize(levels, 8))
        for g in range(8):
            far = levels[np.abs(levels - a[p, g]) >= 10]
            a[p, g + 8] = far[np.random.randint(len(far))]
    return np.exp2(a.ravel()).repeat(32)


def f64(x):
    return np.asarray(x).astype(np.float64)


def striped(idx):
    return np.tile(idx.reshape(-1, 16).T, (8, 1)).astype(np.uint16)


def unstriped(offs):
    return offs[:16].T.reshape(-1).astype(np.int64)


def silu(v):
    return v / (1.0 + np.exp(-np.maximum(v, -700.0)))


K, T, D, S, V, N = 512, 2048, 4, 1024, 512, 128


def setup_inputs():
    n = np.random.standard_normal
    s = mx_kscale(K)[:, None]
    return {
        "xT": (n((K, T)) * s).astype(np.float32),
        "w": (n((K, N)) / np.sqrt(K) / s).astype(np.float32),
        "b": (0.3 * n((N, 1))).astype(np.float32),
        "gate": np.tile(np.random.uniform(0.2, 1.0, (D, 1, V)) / np.sqrt(D), (1, N, 1)).astype(np.float32),
        "offs": striped(np.random.permutation(T)[:S]),
        "pos1": striped(np.random.permutation(S)[:V]),
        "pos2": striped(np.random.permutation(S)[:V]),
        "pos3": striped(np.random.permutation(S)[:V]),
        "pos4": striped(np.random.permutation(S)[:V]),
    }


def reference(xT, w, b, gate, offs, pos1, pos2, pos3, pos4):
    idx = unstriped(offs)
    xq = mxq(f64(xT)[:, idx], 0, "e4m3")
    y = mxq(f64(w), 0, "e4m3").T @ xq
    y = silu(y + f64(b))
    return sum(f64(gate[d]) * y[:, unstriped(p)] for d, p in enumerate((pos1, pos2, pos3, pos4)))

@@ -1,0 +1,149 @@
+from contextlib import ExitStack
+
+import concourse.mybir as mybir
+
+K, T, D, S, V, N = 512, 2048, 4, 1024, 512, 128
+P = 128
+FLOPS = 2 * K * N * S
+
+F32 = mybir.dt.float32
+BF16 = mybir.dt.bfloat16
+U32 = mybir.dt.uint32
+U16 = mybir.dt.uint16
+U8 = mybir.dt.uint8
+FP8X4 = mybir.dt.float8_e4m3fn_x4
+COPY = mybir.ActivationFunctionType.Copy
+SILU = mybir.ActivationFunctionType.Silu
+MULT = mybir.AluOpType.mult
+
+CHUNKS = (
+    (0, 0, 1024, 704),
+    (0, 1024, 1024, 704),
+    (1, 0, 512, 0),
+    (1, 512, 512, 0),
+    (1, 1024, 512, 512),
+    (1, 1536, 512, 352),
+)
+
+
+def tile_picked_sub_lin_silu_sub_e_kernel(
+    tc, xT, w, b, gate, offs, pos1, pos2, pos3, pos4, out
+):
+    nc = tc.nc
+    with ExitStack() as ctx:
+        keep = ctx.enter_context(tc.tile_pool(name="keep", bufs=1))
+        psum = ctx.enter_context(tc.psum_pool(name="psum", bufs=1))
+
+        warm = keep.tile([P, 1], F32, name="warm")
+        warmed = keep.tile([P, 1], F32, name="warmed")
+        nc.gpsimd.memset(warm[:], 0.0)
+        nc.scalar.activation(warmed[:], warm[:], SILU)
+
+        x_rows = xT.rearrange("(p u e) t -> p u e t", u=2, e=2)
+        raws = []
+        offs_t = keep.tile([P, S // 16], U16, name="offs_t")
+        for i, (u, t0, n, nv) in enumerate(CHUNKS):
+            raw = keep.tile([P, 2, n], F32, name=f"raw{i}")
+            nc.sync.dma_start(raw[:], x_rows[:, u, :, t0 : t0 + n])
+            raws.append(raw)
+            if i == 0:
+                nc.sync.dma_start(offs_t[:], offs)
+        w_raw = keep.tile([P, 4, N], F32, name="w_raw")
+        nc.sync.dma_start(w_raw[:], w.rearrange("(p j) n -> p j n", j=4))
+        b_t = keep.tile([P, 1], F32, name="b_t")
+        nc.sync.dma_start(b_t[:], b)
+        pos_ts, gate_ts = [], []
+        for d, pos in enumerate((pos1, pos2, pos3, pos4)):
+            pos_t = keep.tile([P, V // 16], U16, name=f"pos_t{d}")
+            nc.sync.dma_start(pos_t[:], pos)
+            gate_t = keep.tile([P, V], F32, name=f"gate_t{d}")
+            nc.sync.dma_start(gate_t[:], gate[d])
+            pos_ts.append(pos_t)
+            gate_ts.append(gate_t)
+
+        pairs = [keep.tile([P, T, 2], BF16, name=f"pair{u}", align_bytes=64) for u in (0, 1)]
+        picked = keep.tile([P, S * 4], BF16, name="picked", align_bytes=64)
+        words = picked[:].bitcast(U32).rearrange("p (s u) -> p s u", u=2)
+        windows = [pairs[u][:].rearrange("p t e -> p (t e)").bitcast(U32) for u in (0, 1)]
+
+        def round_chunk(i):
+            u, t0, n, nv = CHUNKS[i]
+            src = raws[i][:].rearrange("p e t -> p t e")
+            if nv > 0:
+                nc.vector.tensor_copy(pairs[u][:, t0 : t0 + nv, :], src[:, 0:nv, :])
+            if nv < n:
+                nc.scalar.activation(pairs[u][:, t0 + nv : t0 + n, :], src[:, nv:n, :], COPY)
+
+        def gather(u, s0, n):
+            nc.vector.tensor_copy(
+                words[:, s0 : s0 + n, u], windows[u].indirect(offs_t[:, s0 // 16 : (s0 + n) // 16])
+            )
+
+        round_chunk(0)
+        round_chunk(1)
+        gather(0, 0, S)
+        for i in (2, 3, 4, 5):
+            round_chunk(i)
+
+        w_pack = keep.tile([P, N, 4], BF16, name="w_pack", align_bytes=64)
+        nc.scalar.activation(w_pack[:], w_raw[:].rearrange("p j n -> p n j"), COPY)
+        w_codes = keep.tile([P, N], U32, name="w_codes", align_bytes=64)
+        w_scales = keep.tile([P, N], U8, name="w_scales", align_bytes=64)
+        x_codes = keep.tile([P, S], U32, name="x_codes", align_bytes=64)
+        x_scales = keep.tile([P, S], U8, name="x_scales", align_bytes=64)
+        y = keep.tile([P, S], F32, name="y", align_bytes=64)
+
+        def quantize(s0, n):
+            nc.vector.quantize_mx(
+                out=x_codes[:, s0 : s0 + n].bitcast(FP8X4),
+                scales=x_scales[:, s0 : s0 + n],
+                in_=picked[:, 4 * s0 : 4 * (s0 + n)],
+            )
+
+        def layer(s0, n):
+            acc = psum.tile([P, n], F32, name=f"acc{s0}")
+            nc.tensor.matmul_mx(
+                out=acc[:],
+                lhsT=w_codes[:].bitcast(FP8X4),
+                lhsT_scale=w_scales[:],
+                rhs=x_codes[:, s0 : s0 + n].bitcast(FP8X4),
+                rhs_scale=x_scales[:, s0 : s0 + n],
+                start=True,
+                stop=True,
+            )
+            nc.scalar.activation(y[:, s0 : s0 + n], acc[:], SILU, bias=b_t[:])
+
+        gather(1, 0, 512)
+        nc.vector.quantize_mx(
+            out=w_codes[:].bitcast(FP8X4),
+            scales=w_scales[:],
+            in_=w_pack[:].rearrange("p n j -> p (n j)"),
+        )
+        gather(1, 512, 256)
+        quantize(0, 512)
+        layer(0, 512)
+        gather(1, 768, 256)
+        quantize(512, 256)
+        layer(512, 256)
+        quantize(768, 256)
+        layer(768, 256)
+
+        terms = [keep.tile([P, V], F32, name=f"term{d}") for d in range(D)]
+        sum01 = keep.tile([P, V], F32, name="sum01")
+        sum012 = keep.tile([P, V], F32, name="sum012")
+        total = keep.tile([P, V], F32, name="total")
+
+        def neighbour(d):
+            nc.vector.tensor_tensor(terms[d][:], y[:].indirect(pos_ts[d][:]), gate_ts[d][:], MULT)
+
+        neighbour(0)
+        neighbour(1)
+        neighbour(2)
+        nc.vector.tensor_add(sum01[:], terms[0][:], terms[1][:])
+        neighbour(3)
+        halves = (slice(0, V // 2), slice(V // 2, V))
+        for h in halves:
+            nc.vector.tensor_add(sum012[:, h], sum01[:, h], terms[2][:, h])
+        for h in halves:
+            nc.vector.tensor_add(total[:, h], sum012[:, h], terms[3][:, h])
+            nc.sync.dma_start(out[:, h], total[:, h])

@@ -16,14 +16,12 @@ COPY = mybir.ActivationFunctionType.Copy
 SILU = mybir.ActivationFunctionType.Silu
 MULT = mybir.AluOpType.mult
 
-CHUNKS = (
-    (0, 0, 1024, 704),
-    (0, 1024, 1024, 704),
-    (1, 0, 512, 0),
-    (1, 512, 512, 0),
-    (1, 1024, 512, 512),
-    (1, 1536, 512, 352),
-)
+NV = 512
+K2_CHUNKS = ((0, 1024, 0), (1024, 1024, 0))
+PAIR_CHUNKS = ((0, 1024, 768), (1024, 512, 384), (1536, 256, 176), (1792, 256, 160))
+K3_CHUNKS = ((0, 1024, 0), (1024, 512, 0), (1536, 256, 0), (1792, 256, 0))
+K3_GATHERS = (256, 256)
+PIECES = (256, 256, 256, 128, 128)
 
 
 def tile_picked_sub_lin_silu_sub_e_kernel(
@@ -32,6 +30,7 @@ def tile_picked_sub_lin_silu_sub_e_kernel(
     nc = tc.nc
     with ExitStack() as ctx:
         keep = ctx.enter_context(tc.tile_pool(name="keep", bufs=1))
+        turns = ctx.enter_context(tc.tile_pool(name="turns", bufs=1))
         psum = ctx.enter_context(tc.psum_pool(name="psum", bufs=1))
 
         warm = keep.tile([P, 1], F32, name="warm")
@@ -39,94 +38,99 @@ def tile_picked_sub_lin_silu_sub_e_kernel(
         nc.gpsimd.memset(warm[:], 0.0)
         nc.scalar.activation(warmed[:], warm[:], SILU)
 
-        x_rows = xT.rearrange("(p u e) t -> p u e t", u=2, e=2)
-        raws = []
+        x_rows = xT.rearrange("(p j) t -> p j t", j=4)
         offs_t = keep.tile([P, S // 16], U16, name="offs_t")
-        for i, (u, t0, n, nv) in enumerate(CHUNKS):
-            raw = keep.tile([P, 2, n], F32, name=f"raw{i}")
-            nc.sync.dma_start(raw[:], x_rows[:, u, :, t0 : t0 + n])
-            raws.append(raw)
+        single2 = keep.tile([P, T], F32, name="single2", align_bytes=64)
+        single3 = keep.tile([P, T], F32, name="single3", align_bytes=64)
+        raws = []
+        for i, (t0, n, nv) in enumerate(K2_CHUNKS):
+            nc.sync.dma_start(single2[:, t0 : t0 + n], x_rows[:, 2, t0 : t0 + n])
             if i == 0:
                 nc.sync.dma_start(offs_t[:], offs)
+        for i, (t0, n, nv) in enumerate(PAIR_CHUNKS):
+            raw = keep.tile([P, 2, n], F32, name=f"raw{i}")
+            nc.sync.dma_start(raw[:], x_rows[:, 0:2, t0 : t0 + n])
+            raws.append(raw)
+        for t0, n, nv in K3_CHUNKS:
+            nc.sync.dma_start(single3[:, t0 : t0 + n], x_rows[:, 3, t0 : t0 + n])
         w_raw = keep.tile([P, 4, N], F32, name="w_raw")
         nc.sync.dma_start(w_raw[:], w.rearrange("(p j) n -> p j n", j=4))
         b_t = keep.tile([P, 1], F32, name="b_t")
         nc.sync.dma_start(b_t[:], b)
-        pos_ts, gate_ts = [], []
+        gate_t = keep.tile([P, D, V], F32, name="gate_t")
+        nc.sync.dma_start(gate_t[:], gate.rearrange("d p v -> p d v"))
+        pos_ts = []
         for d, pos in enumerate((pos1, pos2, pos3, pos4)):
             pos_t = keep.tile([P, V // 16], U16, name=f"pos_t{d}")
             nc.sync.dma_start(pos_t[:], pos)
-            gate_t = keep.tile([P, V], F32, name=f"gate_t{d}")
-            nc.sync.dma_start(gate_t[:], gate[d])
             pos_ts.append(pos_t)
-            gate_ts.append(gate_t)
 
-        pairs = [keep.tile([P, T, 2], BF16, name=f"pair{u}", align_bytes=64) for u in (0, 1)]
+        pair = keep.tile([P, T, 2], BF16, name="pair", align_bytes=64)
+        rounded2 = keep.tile([P, T], BF16, name="rounded2", align_bytes=64)
+        rounded3 = turns.tile([P, T], BF16, name="rounded3", tag="late", align_bytes=64)
         picked = keep.tile([P, S * 4], BF16, name="picked", align_bytes=64)
+        values = picked[:].rearrange("p (s j) -> p s j", j=4)
         words = picked[:].bitcast(U32).rearrange("p (s u) -> p s u", u=2)
-        windows = [pairs[u][:].rearrange("p t e -> p (t e)").bitcast(U32) for u in (0, 1)]
+        pair_window = pair[:].rearrange("p t e -> p (t e)").bitcast(U32)
 
-        def round_chunk(i):
-            u, t0, n, nv = CHUNKS[i]
-            src = raws[i][:].rearrange("p e t -> p t e")
+        def round_split(dst, src, t0, n, nv):
             if nv > 0:
-                nc.vector.tensor_copy(pairs[u][:, t0 : t0 + nv, :], src[:, 0:nv, :])
+                nc.vector.tensor_copy(dst[:, t0 : t0 + nv], src[:, 0:nv])
             if nv < n:
-                nc.scalar.activation(pairs[u][:, t0 + nv : t0 + n, :], src[:, nv:n, :], COPY)
+                nc.scalar.activation(dst[:, t0 + nv : t0 + n], src[:, nv:n], COPY)
 
-        def gather(u, s0, n):
-            nc.vector.tensor_copy(
-                words[:, s0 : s0 + n, u], windows[u].indirect(offs_t[:, s0 // 16 : (s0 + n) // 16])
-            )
+        def entries(s0, s1):
+            return offs_t[:, s0 // 16 : s1 // 16]
 
-        round_chunk(0)
-        round_chunk(1)
-        gather(0, 0, S)
-        for i in (2, 3, 4, 5):
-            round_chunk(i)
+        for t0, n, nv in K2_CHUNKS:
+            round_split(rounded2, single2[:, t0 : t0 + n], t0, n, nv)
+        nc.vector.tensor_copy(values[:, 0:NV, 2], single2[:].indirect(entries(0, NV)))
+        nc.scalar.activation(values[:, NV:S, 2], rounded2[:].indirect(entries(NV, S)), COPY)
+        for raw, (t0, n, nv) in zip(raws, PAIR_CHUNKS):
+            round_split(pair, raw[:].rearrange("p e t -> p t e"), t0, n, nv)
+        nc.vector.tensor_copy(words[:, :, 0], pair_window.indirect(offs_t[:]))
+        for t0, n, nv in K3_CHUNKS:
+            round_split(rounded3, single3[:, t0 : t0 + n], t0, n, nv)
+        s0 = 0
+        for n in K3_GATHERS:
+            nc.vector.tensor_copy(values[:, s0 : s0 + n, 3], single3[:].indirect(entries(s0, s0 + n)))
+            s0 += n
+        nc.scalar.activation(values[:, NV:S, 3], rounded3[:].indirect(entries(NV, S)), COPY)
 
         w_pack = keep.tile([P, N, 4], BF16, name="w_pack", align_bytes=64)
-        nc.scalar.activation(w_pack[:], w_raw[:].rearrange("p j n -> p n j"), COPY)
+        nc.vector.tensor_copy(w_pack[:], w_raw[:].rearrange("p j n -> p n j"))
         w_codes = keep.tile([P, N], U32, name="w_codes", align_bytes=64)
         w_scales = keep.tile([P, N], U8, name="w_scales", align_bytes=64)
         x_codes = keep.tile([P, S], U32, name="x_codes", align_bytes=64)
         x_scales = keep.tile([P, S], U8, name="x_scales", align_bytes=64)
-        y = keep.tile([P, S], F32, name="y", align_bytes=64)
+        y = turns.tile([P, S], F32, name="y", tag="late", align_bytes=64)
 
-        def quantize(s0, n):
+        s0 = 0
+        for i, n in enumerate(PIECES):
+            cols = slice(s0, s0 + n)
             nc.vector.quantize_mx(
-                out=x_codes[:, s0 : s0 + n].bitcast(FP8X4),
-                scales=x_scales[:, s0 : s0 + n],
+                out=x_codes[:, cols].bitcast(FP8X4),
+                scales=x_scales[:, cols],
                 in_=picked[:, 4 * s0 : 4 * (s0 + n)],
             )
-
-        def layer(s0, n):
+            if i == 0:
+                nc.vector.quantize_mx(
+                    out=w_codes[:].bitcast(FP8X4),
+                    scales=w_scales[:],
+                    in_=w_pack[:].rearrange("p n j -> p (n j)"),
+                )
             acc = psum.tile([P, n], F32, name=f"acc{s0}")
             nc.tensor.matmul_mx(
                 out=acc[:],
                 lhsT=w_codes[:].bitcast(FP8X4),
                 lhsT_scale=w_scales[:],
-                rhs=x_codes[:, s0 : s0 + n].bitcast(FP8X4),
-                rhs_scale=x_scales[:, s0 : s0 + n],
+                rhs=x_codes[:, cols].bitcast(FP8X4),
+                rhs_scale=x_scales[:, cols],
                 start=True,
                 stop=True,
             )
-            nc.scalar.activation(y[:, s0 : s0 + n], acc[:], SILU, bias=b_t[:])
-
-        gather(1, 0, 512)
-        nc.vector.quantize_mx(
-            out=w_codes[:].bitcast(FP8X4),
-            scales=w_scales[:],
-            in_=w_pack[:].rearrange("p n j -> p (n j)"),
-        )
-        gather(1, 512, 256)
-        quantize(0, 512)
-        layer(0, 512)
-        gather(1, 768, 256)
-        quantize(512, 256)
-        layer(512, 256)
-        quantize(768, 256)
-        layer(768, 256)
+            nc.scalar.activation(y[:, cols], acc[:], SILU, bias=b_t[:])
+            s0 += n
 
         terms = [keep.tile([P, V], F32, name=f"term{d}") for d in range(D)]
         sum01 = keep.tile([P, V], F32, name="sum01")
@@ -134,7 +138,7 @@ def tile_picked_sub_lin_silu_sub_e_kernel(
         total = keep.tile([P, V], F32, name="total")
 
         def neighbour(d):
-            nc.vector.tensor_tensor(terms[d][:], y[:].indirect(pos_ts[d][:]), gate_ts[d][:], MULT)
+            nc.vector.tensor_tensor(terms[d][:], y[:].indirect(pos_ts[d][:]), gate_t[:, d, :], MULT)
 
         neighbour(0)
         neighbour(1)

from contextlib import ExitStack

import concourse.mybir as mybir

K, T, D, S, V, N = 512, 2048, 4, 1024, 512, 128
P = 128
FLOPS = 2 * K * N * S

F32 = mybir.dt.float32
BF16 = mybir.dt.bfloat16
U32 = mybir.dt.uint32
U16 = mybir.dt.uint16
U8 = mybir.dt.uint8
FP8X4 = mybir.dt.float8_e4m3fn_x4
COPY = mybir.ActivationFunctionType.Copy
SILU = mybir.ActivationFunctionType.Silu
MULT = mybir.AluOpType.mult

NV = 512
K2_CHUNKS = ((0, 1024, 0), (1024, 1024, 0))
PAIR_CHUNKS = ((0, 1024, 768), (1024, 512, 384), (1536, 256, 176), (1792, 256, 160))
K3_CHUNKS = ((0, 1024, 0), (1024, 512, 0), (1536, 256, 0), (1792, 256, 0))
K3_GATHERS = (256, 256)
PIECES = (256, 256, 256, 128, 128)


def tile_picked_sub_lin_silu_sub_e_kernel(
    tc, xT, w, b, gate, offs, pos1, pos2, pos3, pos4, out
):
    nc = tc.nc
    with ExitStack() as ctx:
        keep = ctx.enter_context(tc.tile_pool(name="keep", bufs=1))
        turns = ctx.enter_context(tc.tile_pool(name="turns", bufs=1))
        psum = ctx.enter_context(tc.psum_pool(name="psum", bufs=1))

        warm = keep.tile([P, 1], F32, name="warm")
        warmed = keep.tile([P, 1], F32, name="warmed")
        nc.gpsimd.memset(warm[:], 0.0)
        nc.scalar.activation(warmed[:], warm[:], SILU)

        x_rows = xT.rearrange("(p j) t -> p j t", j=4)
        offs_t = keep.tile([P, S // 16], U16, name="offs_t")
        single2 = keep.tile([P, T], F32, name="single2", align_bytes=64)
        single3 = keep.tile([P, T], F32, name="single3", align_bytes=64)
        raws = []
        for i, (t0, n, nv) in enumerate(K2_CHUNKS):
            nc.sync.dma_start(single2[:, t0 : t0 + n], x_rows[:, 2, t0 : t0 + n])
            if i == 0:
                nc.sync.dma_start(offs_t[:], offs)
        for i, (t0, n, nv) in enumerate(PAIR_CHUNKS):
            raw = keep.tile([P, 2, n], F32, name=f"raw{i}")
            nc.sync.dma_start(raw[:], x_rows[:, 0:2, t0 : t0 + n])
            raws.append(raw)
        for t0, n, nv in K3_CHUNKS:
            nc.sync.dma_start(single3[:, t0 : t0 + n], x_rows[:, 3, t0 : t0 + n])
        w_raw = keep.tile([P, 4, N], F32, name="w_raw")
        nc.sync.dma_start(w_raw[:], w.rearrange("(p j) n -> p j n", j=4))
        b_t = keep.tile([P, 1], F32, name="b_t")
        nc.sync.dma_start(b_t[:], b)
        gate_t = keep.tile([P, D, V], F32, name="gate_t")
        nc.sync.dma_start(gate_t[:], gate.rearrange("d p v -> p d v"))
        pos_ts = []
        for d, pos in enumerate((pos1, pos2, pos3, pos4)):
            pos_t = keep.tile([P, V // 16], U16, name=f"pos_t{d}")
            nc.sync.dma_start(pos_t[:], pos)
            pos_ts.append(pos_t)

        pair = keep.tile([P, T, 2], BF16, name="pair", align_bytes=64)
        rounded2 = keep.tile([P, T], BF16, name="rounded2", align_bytes=64)
        rounded3 = turns.tile([P, T], BF16, name="rounded3", tag="late", align_bytes=64)
        picked = keep.tile([P, S * 4], BF16, name="picked", align_bytes=64)
        values = picked[:].rearrange("p (s j) -> p s j", j=4)
        words = picked[:].bitcast(U32).rearrange("p (s u) -> p s u", u=2)
        pair_window = pair[:].rearrange("p t e -> p (t e)").bitcast(U32)

        def round_split(dst, src, t0, n, nv):
            if nv > 0:
                nc.vector.tensor_copy(dst[:, t0 : t0 + nv], src[:, 0:nv])
            if nv < n:
                nc.scalar.activation(dst[:, t0 + nv : t0 + n], src[:, nv:n], COPY)

        def entries(s0, s1):
            return offs_t[:, s0 // 16 : s1 // 16]

        for t0, n, nv in K2_CHUNKS:
            round_split(rounded2, single2[:, t0 : t0 + n], t0, n, nv)
        nc.vector.tensor_copy(values[:, 0:NV, 2], single2[:].indirect(entries(0, NV)))
        nc.scalar.activation(values[:, NV:S, 2], rounded2[:].indirect(entries(NV, S)), COPY)
        for raw, (t0, n, nv) in zip(raws, PAIR_CHUNKS):
            round_split(pair, raw[:].rearrange("p e t -> p t e"), t0, n, nv)
        nc.vector.tensor_copy(words[:, :, 0], pair_window.indirect(offs_t[:]))
        for t0, n, nv in K3_CHUNKS:
            round_split(rounded3, single3[:, t0 : t0 + n], t0, n, nv)
        s0 = 0
        for n in K3_GATHERS:
            nc.vector.tensor_copy(values[:, s0 : s0 + n, 3], single3[:].indirect(entries(s0, s0 + n)))
            s0 += n
        nc.scalar.activation(values[:, NV:S, 3], rounded3[:].indirect(entries(NV, S)), COPY)

        w_pack = keep.tile([P, N, 4], BF16, name="w_pack", align_bytes=64)
        nc.vector.tensor_copy(w_pack[:], w_raw[:].rearrange("p j n -> p n j"))
        w_codes = keep.tile([P, N], U32, name="w_codes", align_bytes=64)
        w_scales = keep.tile([P, N], U8, name="w_scales", align_bytes=64)
        x_codes = keep.tile([P, S], U32, name="x_codes", align_bytes=64)
        x_scales = keep.tile([P, S], U8, name="x_scales", align_bytes=64)
        y = turns.tile([P, S], F32, name="y", tag="late", align_bytes=64)

        s0 = 0
        for i, n in enumerate(PIECES):
            cols = slice(s0, s0 + n)
            nc.vector.quantize_mx(
                out=x_codes[:, cols].bitcast(FP8X4),
                scales=x_scales[:, cols],
                in_=picked[:, 4 * s0 : 4 * (s0 + n)],
            )
            if i == 0:
                nc.vector.quantize_mx(
                    out=w_codes[:].bitcast(FP8X4),
                    scales=w_scales[:],
                    in_=w_pack[:].rearrange("p n j -> p (n j)"),
                )
            acc = psum.tile([P, n], F32, name=f"acc{s0}")
            nc.tensor.matmul_mx(
                out=acc[:],
                lhsT=w_codes[:].bitcast(FP8X4),
                lhsT_scale=w_scales[:],
                rhs=x_codes[:, cols].bitcast(FP8X4),
                rhs_scale=x_scales[:, cols],
                start=True,
                stop=True,
            )
            nc.scalar.activation(y[:, cols], acc[:], SILU, bias=b_t[:])
            s0 += n

        terms = [keep.tile([P, V], F32, name=f"term{d}") for d in range(D)]
        sum01 = keep.tile([P, V], F32, name="sum01")
        sum012 = keep.tile([P, V], F32, name="sum012")
        total = keep.tile([P, V], F32, name="total")

        def neighbour(d):
            nc.vector.tensor_tensor(terms[d][:], y[:].indirect(pos_ts[d][:]), gate_t[:, d, :], MULT)

        neighbour(0)
        neighbour(1)
        neighbour(2)
        nc.vector.tensor_add(sum01[:], terms[0][:], terms[1][:])
        neighbour(3)
        halves = (slice(0, V // 2), slice(V // 2, V))
        for h in halves:
            nc.vector.tensor_add(sum012[:, h], sum01[:, h], terms[2][:, h])
        for h in halves:
            nc.vector.tensor_add(total[:, h], sum012[:, h], terms[3][:, h])
            nc.sync.dma_start(out[:, h], total[:, h])
